import numpy as np
import ml_dtypes


def mxq(x, axis, fmt="e4m3"):
    dtype, down = {"e4m3": (ml_dtypes.float8_e4m3fn, 7), "e5m2": (ml_dtypes.float8_e5m2, 14)}[fmt]
    v = np.moveaxis(np.asarray(x, np.float32).astype(ml_dtypes.bfloat16).astype(np.float64), axis, -1)
    blocks = v.reshape(v.shape[:-1] + (-1, 32))
    amax = np.abs(blocks).max(-1, keepdims=True)
    byte = np.maximum(np.where(amax > 0, np.frexp(amax)[1] - 1 + 127, 0) - down, 1)
    scale = np.exp2(byte - 127.0)
    codes = (blocks / scale).astype(np.float32).astype(dtype).astype(np.float64)
    return np.moveaxis((codes * scale).reshape(v.shape), -1, axis)


WIDE = False


def mx_kscale(k):
    if not WIDE:
        return np.ones(k)
    levels = np.array([10, -10, 5, -5, 0])
    if k % 512:
        return np.exp2(np.random.permutation(np.resize(levels, k // 32))).repeat(32)
    a = np.empty((k // 512, 16))
    for p in range(k // 512):
        a[p, :8] = np.random.permutation(np.resize(levels, 8))
        for g in range(8):
            far = levels[np.abs(levels - a[p, g]) >= 10]
            a[p, g + 8] = far[np.random.randint(len(far))]
    return np.exp2(a.ravel()).repeat(32)


def f64(x):
    return np.asarray(x).astype(np.float64)


def striped(idx):
    return np.tile(idx.reshape(-1, 16).T, (8, 1)).astype(np.uint16)


def unstriped(offs):
    return offs[:16].T.reshape(-1).astype(np.int64)


def pack_weight(w):
    k, n = w.shape
    w = f64(np.asarray(w, np.float32).astype(ml_dtypes.bfloat16)).reshape(k // 32, 32, n)
    amax = np.abs(w).max(1)
    byte = np.clip(np.where(amax > 0, np.frexp(amax)[1] - 1 + 127 - 7, 1), 1, 254)
    scaled = (w * np.exp2(127.0 - byte)[:, None, :]).reshape(k, n).astype(np.float32)
    words = np.ascontiguousarray(scaled.reshape(k // 512, 128, 4, n).transpose(0, 1, 3, 2)).astype(ml_dtypes.float8_e4m3fn).view(np.uint8)
    return words, np.ascontiguousarray(byte.astype(np.uint8).reshape(k // 512, 16, n))


def unpack_weight(words, scales):
    g, p, n, _ = words.shape
    vals = np.ascontiguousarray(words).view(ml_dtypes.float8_e4m3fn).astype(np.float64) * np.repeat(np.exp2(scales.astype(np.float64) - 127.0), 8, axis=1)[..., None]
    return vals.transpose(0, 1, 3, 2).reshape(g * 512, n)


def sigmoid(v):
    return 1.0 / (1.0 + np.exp(-np.maximum(v, -700.0)))


K, T, S, N, U = 1024, 2048, 512, 256, 1024


def setup_inputs():
    n = np.random.standard_normal
    s = mx_kscale(K)[:, None]
    packed_xT = pack_weight(n((K, T)) * s)
    return {
        "x_words": packed_xT[0],
        "x_scales": packed_xT[1],
        "cell": (n((N, U))).astype(np.float32),
        "w1": (n((K, N)) / np.sqrt(K) / s).astype(np.float32),
        "w2": (n((K, N)) / np.sqrt(K) / s).astype(np.float32),
        "w3": (n((K, N)) / np.sqrt(K) / s).astype(np.float32),
        "peep": (0.5 * n((N, 1))).astype(np.float32),
        "offs": striped(np.random.permutation(T)[:S]),
        "slot": striped(np.random.permutation(U)[:S]),
    }


def reference(x_words, x_scales, cell, w1, w2, w3, peep, offs, slot):
    xq = unpack_weight(x_words, x_scales)[:, unstriped(offs)]
    rr = sigmoid(mxq(f64(w3), 0, "e4m3").T @ xq)
    y = mxq(f64(w2), 0, "e4m3").T @ xq
    old = f64(cell)[:, unstriped(slot)]
    f = sigmoid((mxq(f64(w1), 0, "e4m3").T @ xq) + f64(peep) * old)
    new = y + f * (old - y)
    return rr * np.tanh(new)

@@ -1,0 +1,202 @@
+from contextlib import ExitStack
+
+import concourse.mybir as mybir
+
+K, T, S, N, U = 1024, 2048, 512, 256, 1024
+FLOPS = 3 * 2 * K * N * S
+
+F32 = mybir.dt.float32
+BF16 = mybir.dt.bfloat16
+I32 = mybir.dt.int32
+U32 = mybir.dt.uint32
+U16 = mybir.dt.uint16
+U8 = mybir.dt.uint8
+FP8X4 = mybir.dt.float8_e4m3fn_x4
+ALU = mybir.AluOpType
+ACT = mybir.ActivationFunctionType
+
+P = 128
+PACK = 4
+PASSES = K // (P * PACK)
+BLOCKS = N // P
+
+
+def tile_picked_ysru_tanh_p_kernel(tc, x_words, x_scales, cell, w1, w2, w3, peep, offs, slot, out):
+    nc = tc.nc
+    weights = {1: w1, 2: w2, 3: w3}
+    with ExitStack() as ctx:
+        keep = ctx.enter_context(tc.tile_pool(name="keep", bufs=1))
+        psum = ctx.enter_context(tc.psum_pool(name="psum", bufs=1))
+
+        offs_sb = keep.tile([P, S // 16], U16, name="offs_sb")
+        slot_sb = keep.tile([P, S // 16], U16, name="slot_sb")
+        peep_sb = keep.tile([P, BLOCKS], F32, name="peep_sb")
+        warm = keep.tile([P, 2], F32, name="warm")
+        xs = keep.tile([P, T], U8, name="xs", align_bytes=64)
+        xs_g = keep.tile([P, S], U8, name="xs_g", align_bytes=64)
+        xw = [keep.tile([P, T], U32, name=f"xw{g}", align_bytes=64) for g in range(PASSES)]
+        xw_g = [keep.tile([P, S], U32, name=f"xw_g{g}", align_bytes=64) for g in range(PASSES)]
+        cell_sb = [keep.tile([P, U], F32, name=f"cell{b}", align_bytes=64) for b in range(BLOCKS)]
+        keys = [(i, g) for i in weights for g in range(PASSES)]
+        raw = {k: keep.tile([P, PACK, N], F32, name=f"raw{k[0]}{k[1]}", align_bytes=64) for k in keys}
+        kb = [(i, g, b) for i, g in keys for b in range(BLOCKS)]
+        grouped = {k: keep.tile([P, P, PACK], BF16, name="grp%d%d%d" % k, align_bytes=64) for k in kb}
+        codes = {k: keep.tile([P, P], U32, name="cod%d%d%d" % k, align_bytes=64) for k in kb}
+        scales = {k: keep.tile([P, P], U8, name="scl%d%d%d" % k, align_bytes=64) for k in kb}
+        acc = {(i, b): psum.tile([P, S], F32, name=f"acc{i}{b}") for i in weights for b in range(BLOCKS)}
+
+        def work(name):
+            return [keep.tile([P, S], F32, name=f"{name}{b}", align_bytes=64) for b in range(BLOCKS)]
+
+        old, pre, forget, admit, kept, fresh, new, squashed, gate, res = (
+            work(n) for n in ("old", "pre", "forget", "admit", "kept", "fresh", "new", "squashed", "gate", "res")
+        )
+
+        def load_x(g):
+            nc.sync.dma_start(xw[g][:].bitcast(I32), x_words[g].rearrange("p n t -> p (n t)").bitcast(I32))
+
+        def load_cell(b):
+            nc.sync.dma_start(cell_sb[b][:], cell[b * P : (b + 1) * P, :])
+
+        def load_w(i, g):
+            rows = weights[i][g * P * PACK : (g + 1) * P * PACK, :]
+            nc.sync.dma_start(raw[i, g][:], rows.rearrange("(p j) n -> p j n", j=PACK))
+
+        def load_scales(eng):
+            for q in range(4):
+                eng.dma_start(xs[32 * q : 32 * q + 8, :].bitcast(I32), x_scales[:, 4 * q : 4 * q + 4, :].bitcast(I32))
+
+        def load_peep(eng):
+            with nc.allow_non_contiguous_dma(reason="one value a partition"):
+                eng.dma_start(peep_sb[:], peep.rearrange("(b p) o -> p (b o)", p=P))
+
+        def gather_x(g):
+            nc.vector.tensor_copy(xw_g[g][:], xw[g][:].indirect(offs_sb[:]))
+
+        def gather_scales():
+            nc.vector.tensor_copy(xs_g[:], xs[:].indirect(offs_sb[:]))
+
+        def gather_cell(b):
+            nc.vector.tensor_copy(old[b][:], cell_sb[b][:].indirect(slot_sb[:]))
+
+        def weave(i, g, b, eng):
+            src = raw[i, g][:, :, b * P : (b + 1) * P].rearrange("p t (c e) -> p c t e", e=4)
+            dst = grouped[i, g, b][:].rearrange("p (c e) t -> p c t e", e=4)
+            if eng == "v":
+                nc.vector.tensor_copy(dst, src)
+            else:
+                nc.scalar.copy(dst, src)
+
+        def quant(i, g, b):
+            nc.vector.quantize_mx(
+                out=codes[i, g, b][:].bitcast(FP8X4),
+                scales=scales[i, g, b][:],
+                in_=grouped[i, g, b][:].rearrange("p n t -> p (n t)"),
+            )
+
+        def product(i, g, b, start, stop):
+            nc.tensor.matmul_mx(
+                out=acc[i, b][:],
+                lhsT=codes[i, g, b][:].bitcast(FP8X4),
+                lhsT_scale=scales[i, g, b][:],
+                rhs=xw_g[g][:].bitcast(FP8X4),
+                rhs_scale=xs_g[4 * g : P, :],
+                start=start,
+                stop=stop,
+            )
+
+        def unit(i, g, engs, first):
+            for b in range(BLOCKS):
+                weave(i, g, b, engs[b])
+            for b in range(BLOCKS):
+                quant(i, g, b)
+            for b in range(BLOCKS):
+                product(i, g, b, first, not first)
+
+        full = slice(0, S)
+
+        def f_pre(b, c=full):
+            nc.vector.scalar_tensor_tensor(pre[b][:, c], old[b][:, c], peep_sb[:, b : b + 1], acc[1, b][:, c], ALU.mult, ALU.add)
+
+        def f_gate(b, c=full):
+            nc.scalar.activation(forget[b][:, c], pre[b][:, c], ACT.Sigmoid)
+
+        def g_gate(b, c=full):
+            nc.scalar.activation(admit[b][:, c], pre[b][:, c], ACT.Sigmoid, scale=-1.0)
+
+        def keep_old(b, c=full):
+            nc.vector.tensor_tensor(kept[b][:, c], old[b][:, c], forget[b][:, c], ALU.mult)
+
+        def admit_new(b, c=full):
+            nc.vector.tensor_tensor(fresh[b][:, c], acc[2, b][:, c], admit[b][:, c], ALU.mult)
+
+        def blend(b, c=full):
+            nc.vector.tensor_tensor(new[b][:, c], kept[b][:, c], fresh[b][:, c], ALU.add)
+
+        def diff(b, c=full):
+            nc.vector.tensor_tensor(kept[b][:, c], old[b][:, c], acc[2, b][:, c], ALU.subtract)
+
+        def scale_diff(b, c=full):
+            nc.vector.tensor_tensor(fresh[b][:, c], kept[b][:, c], forget[b][:, c], ALU.mult)
+
+        def add_y(b, c=full):
+            nc.vector.tensor_tensor(new[b][:, c], fresh[b][:, c], acc[2, b][:, c], ALU.add)
+
+        def squash(b, c=full):
+            nc.scalar.activation(squashed[b][:, c], new[b][:, c], ACT.Tanh)
+
+        def r_gate(b, c=full):
+            nc.scalar.activation(gate[b][:, c], acc[3, b][:, c], ACT.Sigmoid)
+
+        def finish(b, c=full):
+            nc.vector.tensor_tensor(res[b][:, c], squashed[b][:, c], gate[b][:, c], ALU.mult)
+
+        def store(b, c=full, eng=nc.sync):
+            eng.dma_start(out[b * P : (b + 1) * P, c], res[b][:, c])
+
+        nc.vector.memset(xs[:].bitcast(I32), 0)
+        nc.vector.memset(warm[:, 0:1], 0.0)
+        nc.scalar.activation(warm[:, 1:2], warm[:, 0:1], ACT.Sigmoid)
+        nc.sync.dma_start(offs_sb[:], offs)
+        load_x(0)
+        nc.sync.dma_start(slot_sb[:], slot)
+        load_scales(nc.gpsimd)
+        load_peep(nc.gpsimd)
+        load_cell(0)
+        load_w(1, 0)
+        load_x(1)
+        load_w(1, 1)
+        load_cell(1)
+        load_w(2, 0)
+        load_w(2, 1)
+        load_w(3, 0)
+        load_w(3, 1)
+        gather_scales()
+        gather_x(0)
+        gather_cell(0)
+        unit(1, 0, "ss", True)
+        gather_x(1)
+        unit(1, 1, "sv", False)
+        f_pre(0)
+        gather_cell(1)
+        f_gate(0)
+        g_gate(0)
+        f_pre(1)
+        unit(2, 0, "sv", True)
+        keep_old(0)
+        f_gate(1)
+        g_gate(1)
+        unit(2, 1, "sv", False)
+        keep_old(1)
+        admit_new(0)
+        admit_new(1)
+        blend(0)
+        blend(1)
+        unit(3, 0, "ss", True)
+        squash(0)
+        squash(1)
+        unit(3, 1, "sv", False)
+        for b in range(BLOCKS):
+            r_gate(b)
+            finish(b)
+            store(b)

@@ -39,10 +39,7 @@ def tile_picked_ysru_tanh_p_kernel(tc, x_words, x_scales, cell, w1, w2, w3, peep
         cell_sb = [keep.tile([P, U], F32, name=f"cell{b}", align_bytes=64) for b in range(BLOCKS)]
         keys = [(i, g) for i in weights for g in range(PASSES)]
         raw = {k: keep.tile([P, PACK, N], F32, name=f"raw{k[0]}{k[1]}", align_bytes=64) for k in keys}
-        kb = [(i, g, b) for i, g in keys for b in range(BLOCKS)]
-        grouped = {k: keep.tile([P, P, PACK], BF16, name="grp%d%d%d" % k, align_bytes=64) for k in kb}
-        codes = {k: keep.tile([P, P], U32, name="cod%d%d%d" % k, align_bytes=64) for k in kb}
-        scales = {k: keep.tile([P, P], U8, name="scl%d%d%d" % k, align_bytes=64) for k in kb}
+        grouped, codes, scales = {}, {}, {}
         acc = {(i, b): psum.tile([P, S], F32, name=f"acc{i}{b}") for i in weights for b in range(BLOCKS)}
 
         def work(name):
@@ -79,39 +76,55 @@ def tile_picked_ysru_tanh_p_kernel(tc, x_words, x_scales, cell, w1, w2, w3, peep
         def gather_cell(b):
             nc.vector.tensor_copy(old[b][:], cell_sb[b][:].indirect(slot_sb[:]))
 
+        def cols(b):
+            return slice(0, N) if b is None else slice(b * P, (b + 1) * P)
+
         def weave(i, g, b, eng):
-            src = raw[i, g][:, :, b * P : (b + 1) * P].rearrange("p t (c e) -> p c t e", e=4)
-            dst = grouped[i, g, b][:].rearrange("p (c e) t -> p c t e", e=4)
+            width = N if b is None else P
+            tag = f"{i}{g}{b}"
+            grp = keep.tile([P, width, PACK], BF16, name="grp" + tag, align_bytes=64)
+            grouped[i, g, b] = grp
+            src = raw[i, g][:, :, cols(b)].rearrange("p t (c e) -> p c t e", e=4)
+            dst = grp[:].rearrange("p (c e) t -> p c t e", e=4)
             if eng == "v":
                 nc.vector.tensor_copy(dst, src)
             else:
                 nc.scalar.copy(dst, src)
 
         def quant(i, g, b):
+            width = N if b is None else P
+            tag = f"{i}{g}{b}"
+            cod = keep.tile([P, width], U32, name="cod" + tag, align_bytes=64)
+            scl = keep.tile([P, width], U8, name="scl" + tag, align_bytes=64)
             nc.vector.quantize_mx(
-                out=codes[i, g, b][:].bitcast(FP8X4),
-                scales=scales[i, g, b][:],
+                out=cod[:].bitcast(FP8X4),
+                scales=scl[:],
                 in_=grouped[i, g, b][:].rearrange("p n t -> p (n t)"),
             )
+            for c in range(BLOCKS) if b is None else [b]:
+                part = cols(c) if b is None else slice(0, P)
+                codes[i, g, c] = cod[:, part]
+                scales[i, g, c] = scl[:, part]
 
-        def product(i, g, b, start, stop):
+        def product(i, g, b):
             nc.tensor.matmul_mx(
                 out=acc[i, b][:],
-                lhsT=codes[i, g, b][:].bitcast(FP8X4),
-                lhsT_scale=scales[i, g, b][:],
+                lhsT=codes[i, g, b].bitcast(FP8X4),
+                lhsT_scale=scales[i, g, b],
                 rhs=xw_g[g][:].bitcast(FP8X4),
                 rhs_scale=xs_g[4 * g : P, :],
-                start=start,
-                stop=stop,
+                start=(g == 0),
+                stop=(g == PASSES - 1),
             )
 
-        def unit(i, g, engs, first):
-            for b in range(BLOCKS):
-                weave(i, g, b, engs[b])
-            for b in range(BLOCKS):
+        def unit(i, g, engs):
+            parts = [None] if len(engs) == 1 else range(BLOCKS)
+            for b, e in zip(parts, engs):
+                weave(i, g, b, e)
+            for b in parts:
                 quant(i, g, b)
             for b in range(BLOCKS):
-                product(i, g, b, first, not first)
+                product(i, g, b)
 
         full = slice(0, S)
 
@@ -128,10 +141,10 @@ def tile_picked_ysru_tanh_p_kernel(tc, x_words, x_scales, cell, w1, w2, w3, peep
             nc.vector.tensor_tensor(kept[b][:, c], old[b][:, c], forget[b][:, c], ALU.mult)
 
         def admit_new(b, c=full):
-            nc.vector.tensor_tensor(fresh[b][:, c], acc[2, b][:, c], admit[b][:, c], ALU.mult)
+            nc.vector.scalar_tensor_tensor(fresh[b][:, c], forget[b][:, c], 1.0, acc[2, b][:, c], ALU.subtract, ALU.mult)
 
         def blend(b, c=full):
-            nc.vector.tensor_tensor(new[b][:, c], kept[b][:, c], fresh[b][:, c], ALU.add)
+            nc.vector.tensor_tensor(new[b][:, c], kept[b][:, c], fresh[b][:, c], ALU.subtract)
 
         def diff(b, c=full):
             nc.vector.tensor_tensor(kept[b][:, c], old[b][:, c], acc[2, b][:, c], ALU.subtract)
@@ -154,49 +167,48 @@ def tile_picked_ysru_tanh_p_kernel(tc, x_words, x_scales, cell, w1, w2, w3, peep
         def store(b, c=full, eng=nc.sync):
             eng.dma_start(out[b * P : (b + 1) * P, c], res[b][:, c])
 
-        nc.vector.memset(xs[:].bitcast(I32), 0)
+        nc.gpsimd.memset(xs[:].bitcast(I32), 0)
         nc.vector.memset(warm[:, 0:1], 0.0)
         nc.scalar.activation(warm[:, 1:2], warm[:, 0:1], ACT.Sigmoid)
         nc.sync.dma_start(offs_sb[:], offs)
-        load_x(0)
         nc.sync.dma_start(slot_sb[:], slot)
-        load_scales(nc.gpsimd)
-        load_peep(nc.gpsimd)
+        load_scales(nc.sync)
         load_cell(0)
         load_w(1, 0)
-        load_x(1)
+        load_x(0)
         load_w(1, 1)
+        load_x(1)
         load_cell(1)
         load_w(2, 0)
         load_w(2, 1)
+        load_peep(nc.sync)
         load_w(3, 0)
         load_w(3, 1)
         gather_scales()
-        gather_x(0)
         gather_cell(0)
-        unit(1, 0, "ss", True)
+        gather_x(0)
+        unit(1, 0, "s")
         gather_x(1)
-        unit(1, 1, "sv", False)
-        f_pre(0)
+        unit(1, 1, "s")
         gather_cell(1)
-        f_gate(0)
-        g_gate(0)
-        f_pre(1)
-        unit(2, 0, "sv", True)
-        keep_old(0)
-        f_gate(1)
-        g_gate(1)
-        unit(2, 1, "sv", False)
-        keep_old(1)
-        admit_new(0)
-        admit_new(1)
-        blend(0)
-        blend(1)
-        unit(3, 0, "ss", True)
-        squash(0)
-        squash(1)
-        unit(3, 1, "sv", False)
+        unit(2, 0, "sv")
+        unit(2, 1, "sv")
+        for b in range(BLOCKS):
+            f_pre(b)
+        unit(3, 0, "s")
+        unit(3, 1, "vs")
+        for b in range(BLOCKS):
+            f_gate(b)
+        for b in range(BLOCKS):
+            admit_new(b)
+            keep_old(b)
         for b in range(BLOCKS):
             r_gate(b)
-            finish(b)
-            store(b)
+        for b in range(BLOCKS):
+            blend(b)
+        for b in range(BLOCKS):
+            for h in range(2):
+                c = slice(h * 256, (h + 1) * 256)
+                squash(b, c)
+                finish(b, c)
+                store(b, c)

@@ -1,6 +1,7 @@
 from contextlib import ExitStack
 
 import concourse.mybir as mybir
+from concourse.masks import make_identity
 
 K, T, S, N, U = 1024, 2048, 512, 256, 1024
 FLOPS = 3 * 2 * K * N * S
@@ -66,6 +67,17 @@ def tile_picked_ysru_tanh_p_kernel(tc, x_words, x_scales, cell, w1, w2, w3, peep
         def load_peep(eng):
             with nc.allow_non_contiguous_dma(reason="one value a partition"):
                 eng.dma_start(peep_sb[:], peep.rearrange("(b p) o -> p (b o)", p=P))
+
+        ident = keep.tile([P, P], F32, name="ident", align_bytes=64)
+        peep_rows = keep.tile([P, P], F32, name="peep_rows", align_bytes=64)
+        peep_ps = psum.tile([P, P], F32, name="peep_ps")
+
+        def load_peep_rows():
+            nc.sync.dma_start(peep_rows[0:BLOCKS, :], peep.rearrange("(b p) o -> b (p o)", p=P))
+
+        def turn_peep():
+            nc.tensor.transpose(peep_ps[:], peep_rows[:], ident[:])
+            nc.scalar.copy(peep_sb[:], peep_ps[:, 0:BLOCKS])
 
         def gather_x(g):
             nc.vector.tensor_copy(xw_g[g][:], xw[g][:].indirect(offs_sb[:]))
@@ -169,46 +181,52 @@ def tile_picked_ysru_tanh_p_kernel(tc, x_words, x_scales, cell, w1, w2, w3, peep
 
         nc.gpsimd.memset(xs[:].bitcast(I32), 0)
         nc.vector.memset(warm[:, 0:1], 0.0)
+        nc.vector.memset(peep_rows[:], 0.0)
+        make_identity(nc, ident[:])
         nc.scalar.activation(warm[:, 1:2], warm[:, 0:1], ACT.Sigmoid)
         nc.sync.dma_start(offs_sb[:], offs)
-        nc.sync.dma_start(slot_sb[:], slot)
-        load_scales(nc.sync)
-        load_cell(0)
         load_w(1, 0)
+        nc.sync.dma_start(slot_sb[:], slot)
+        load_cell(0)
         load_x(0)
-        load_w(1, 1)
+        load_scales(nc.sync)
         load_x(1)
+        load_w(1, 1)
         load_cell(1)
+        load_peep_rows()
         load_w(2, 0)
         load_w(2, 1)
-        load_peep(nc.sync)
         load_w(3, 0)
         load_w(3, 1)
-        gather_scales()
+        turn_peep()
         gather_cell(0)
         gather_x(0)
-        unit(1, 0, "s")
+        gather_scales()
         gather_x(1)
-        unit(1, 1, "s")
+        unit(1, 0, "s")
+        unit(1, 1, "vv")
         gather_cell(1)
-        unit(2, 0, "sv")
-        unit(2, 1, "sv")
         for b in range(BLOCKS):
             f_pre(b)
-        unit(3, 0, "s")
-        unit(3, 1, "vs")
+        unit(2, 0, "s")
         for b in range(BLOCKS):
             f_gate(b)
+        unit(2, 1, "vv")
+        unit(3, 0, "ss")
+        unit(3, 1, "ss")
+        halves = [slice(h * 256, (h + 1) * 256) for h in range(2)]
         for b in range(BLOCKS):
-            admit_new(b)
             keep_old(b)
         for b in range(BLOCKS):
+            for c in halves:
+                admit_new(b, c)
+            for c in halves:
+                blend(b, c)
+        for b in range(BLOCKS):
             r_gate(b)
-        for b in range(BLOCKS):
-            blend(b)
-        for b in range(BLOCKS):
-            for h in range(2):
-                c = slice(h * 256, (h + 1) * 256)
+            for c in halves:
                 squash(b, c)
+        for b in range(BLOCKS):
+            for c in halves:
                 finish(b, c)
                 store(b, c)

from contextlib import ExitStack

import concourse.mybir as mybir
from concourse.masks import make_identity

K, T, S, N, U = 1024, 2048, 512, 256, 1024
FLOPS = 3 * 2 * K * N * S

F32 = mybir.dt.float32
BF16 = mybir.dt.bfloat16
I32 = mybir.dt.int32
U32 = mybir.dt.uint32
U16 = mybir.dt.uint16
U8 = mybir.dt.uint8
FP8X4 = mybir.dt.float8_e4m3fn_x4
ALU = mybir.AluOpType
ACT = mybir.ActivationFunctionType

P = 128
PACK = 4
PASSES = K // (P * PACK)
BLOCKS = N // P


def tile_picked_ysru_tanh_p_kernel(tc, x_words, x_scales, cell, w1, w2, w3, peep, offs, slot, out):
    nc = tc.nc
    weights = {1: w1, 2: w2, 3: w3}
    with ExitStack() as ctx:
        keep = ctx.enter_context(tc.tile_pool(name="keep", bufs=1))
        psum = ctx.enter_context(tc.psum_pool(name="psum", bufs=1))

        offs_sb = keep.tile([P, S // 16], U16, name="offs_sb")
        slot_sb = keep.tile([P, S // 16], U16, name="slot_sb")
        peep_sb = keep.tile([P, BLOCKS], F32, name="peep_sb")
        warm = keep.tile([P, 2], F32, name="warm")
        xs = keep.tile([P, T], U8, name="xs", align_bytes=64)
        xs_g = keep.tile([P, S], U8, name="xs_g", align_bytes=64)
        xw = [keep.tile([P, T], U32, name=f"xw{g}", align_bytes=64) for g in range(PASSES)]
        xw_g = [keep.tile([P, S], U32, name=f"xw_g{g}", align_bytes=64) for g in range(PASSES)]
        cell_sb = [keep.tile([P, U], F32, name=f"cell{b}", align_bytes=64) for b in range(BLOCKS)]
        keys = [(i, g) for i in weights for g in range(PASSES)]
        raw = {k: keep.tile([P, PACK, N], F32, name=f"raw{k[0]}{k[1]}", align_bytes=64) for k in keys}
        grouped, codes, scales = {}, {}, {}
        acc = {(i, b): psum.tile([P, S], F32, name=f"acc{i}{b}") for i in weights for b in range(BLOCKS)}

        def work(name):
            return [keep.tile([P, S], F32, name=f"{name}{b}", align_bytes=64) for b in range(BLOCKS)]

        old, pre, forget, admit, kept, fresh, new, squashed, gate, res = (
            work(n) for n in ("old", "pre", "forget", "admit", "kept", "fresh", "new", "squashed", "gate", "res")
        )

        def load_x(g):
            nc.sync.dma_start(xw[g][:].bitcast(I32), x_words[g].rearrange("p n t -> p (n t)").bitcast(I32))

        def load_cell(b):
            nc.sync.dma_start(cell_sb[b][:], cell[b * P : (b + 1) * P, :])

        def load_w(i, g):
            rows = weights[i][g * P * PACK : (g + 1) * P * PACK, :]
            nc.sync.dma_start(raw[i, g][:], rows.rearrange("(p j) n -> p j n", j=PACK))

        def load_scales(eng):
            for q in range(4):
                eng.dma_start(xs[32 * q : 32 * q + 8, :].bitcast(I32), x_scales[:, 4 * q : 4 * q + 4, :].bitcast(I32))

        def load_peep(eng):
            with nc.allow_non_contiguous_dma(reason="one value a partition"):
                eng.dma_start(peep_sb[:], peep.rearrange("(b p) o -> p (b o)", p=P))

        ident = keep.tile([P, P], F32, name="ident", align_bytes=64)
        peep_rows = keep.tile([P, P], F32, name="peep_rows", align_bytes=64)
        peep_ps = psum.tile([P, P], F32, name="peep_ps")

        def load_peep_rows():
            nc.sync.dma_start(peep_rows[0:BLOCKS, :], peep.rearrange("(b p) o -> b (p o)", p=P))

        def turn_peep():
            nc.tensor.transpose(peep_ps[:], peep_rows[:], ident[:])
            nc.scalar.copy(peep_sb[:], peep_ps[:, 0:BLOCKS])

        def gather_x(g):
            nc.vector.tensor_copy(xw_g[g][:], xw[g][:].indirect(offs_sb[:]))

        def gather_scales():
            nc.vector.tensor_copy(xs_g[:], xs[:].indirect(offs_sb[:]))

        def gather_cell(b):
            nc.vector.tensor_copy(old[b][:], cell_sb[b][:].indirect(slot_sb[:]))

        def cols(b):
            return slice(0, N) if b is None else slice(b * P, (b + 1) * P)

        def weave(i, g, b, eng):
            width = N if b is None else P
            tag = f"{i}{g}{b}"
            grp = keep.tile([P, width, PACK], BF16, name="grp" + tag, align_bytes=64)
            grouped[i, g, b] = grp
            src = raw[i, g][:, :, cols(b)].rearrange("p t (c e) -> p c t e", e=4)
            dst = grp[:].rearrange("p (c e) t -> p c t e", e=4)
            if eng == "v":
                nc.vector.tensor_copy(dst, src)
            else:
                nc.scalar.copy(dst, src)

        def quant(i, g, b):
            width = N if b is None else P
            tag = f"{i}{g}{b}"
            cod = keep.tile([P, width], U32, name="cod" + tag, align_bytes=64)
            scl = keep.tile([P, width], U8, name="scl" + tag, align_bytes=64)
            nc.vector.quantize_mx(
                out=cod[:].bitcast(FP8X4),
                scales=scl[:],
                in_=grouped[i, g, b][:].rearrange("p n t -> p (n t)"),
            )
            for c in range(BLOCKS) if b is None else [b]:
                part = cols(c) if b is None else slice(0, P)
                codes[i, g, c] = cod[:, part]
                scales[i, g, c] = scl[:, part]

        def product(i, g, b):
            nc.tensor.matmul_mx(
                out=acc[i, b][:],
                lhsT=codes[i, g, b].bitcast(FP8X4),
                lhsT_scale=scales[i, g, b],
                rhs=xw_g[g][:].bitcast(FP8X4),
                rhs_scale=xs_g[4 * g : P, :],
                start=(g == 0),
                stop=(g == PASSES - 1),
            )

        def unit(i, g, engs):
            parts = [None] if len(engs) == 1 else range(BLOCKS)
            for b, e in zip(parts, engs):
                weave(i, g, b, e)
            for b in parts:
                quant(i, g, b)
            for b in range(BLOCKS):
                product(i, g, b)

        full = slice(0, S)

        def f_pre(b, c=full):
            nc.vector.scalar_tensor_tensor(pre[b][:, c], old[b][:, c], peep_sb[:, b : b + 1], acc[1, b][:, c], ALU.mult, ALU.add)

        def f_gate(b, c=full):
            nc.scalar.activation(forget[b][:, c], pre[b][:, c], ACT.Sigmoid)

        def g_gate(b, c=full):
            nc.scalar.activation(admit[b][:, c], pre[b][:, c], ACT.Sigmoid, scale=-1.0)

        def keep_old(b, c=full):
            nc.vector.tensor_tensor(kept[b][:, c], old[b][:, c], forget[b][:, c], ALU.mult)

        def admit_new(b, c=full):
            nc.vector.scalar_tensor_tensor(fresh[b][:, c], forget[b][:, c], 1.0, acc[2, b][:, c], ALU.subtract, ALU.mult)

        def blend(b, c=full):
            nc.vector.tensor_tensor(new[b][:, c], kept[b][:, c], fresh[b][:, c], ALU.subtract)

        def diff(b, c=full):
            nc.vector.tensor_tensor(kept[b][:, c], old[b][:, c], acc[2, b][:, c], ALU.subtract)

        def scale_diff(b, c=full):
            nc.vector.tensor_tensor(fresh[b][:, c], kept[b][:, c], forget[b][:, c], ALU.mult)

        def add_y(b, c=full):
            nc.vector.tensor_tensor(new[b][:, c], fresh[b][:, c], acc[2, b][:, c], ALU.add)

        def squash(b, c=full):
            nc.scalar.activation(squashed[b][:, c], new[b][:, c], ACT.Tanh)

        def r_gate(b, c=full):
            nc.scalar.activation(gate[b][:, c], acc[3, b][:, c], ACT.Sigmoid)

        def finish(b, c=full):
            nc.vector.tensor_tensor(res[b][:, c], squashed[b][:, c], gate[b][:, c], ALU.mult)

        def store(b, c=full, eng=nc.sync):
            eng.dma_start(out[b * P : (b + 1) * P, c], res[b][:, c])

        nc.gpsimd.memset(xs[:].bitcast(I32), 0)
        nc.vector.memset(warm[:, 0:1], 0.0)
        nc.vector.memset(peep_rows[:], 0.0)
        make_identity(nc, ident[:])
        nc.scalar.activation(warm[:, 1:2], warm[:, 0:1], ACT.Sigmoid)
        nc.sync.dma_start(offs_sb[:], offs)
        load_w(1, 0)
        nc.sync.dma_start(slot_sb[:], slot)
        load_cell(0)
        load_x(0)
        load_scales(nc.sync)
        load_x(1)
        load_w(1, 1)
        load_cell(1)
        load_peep_rows()
        load_w(2, 0)
        load_w(2, 1)
        load_w(3, 0)
        load_w(3, 1)
        turn_peep()
        gather_cell(0)
        gather_x(0)
        gather_scales()
        gather_x(1)
        unit(1, 0, "s")
        unit(1, 1, "vv")
        gather_cell(1)
        for b in range(BLOCKS):
            f_pre(b)
        unit(2, 0, "s")
        for b in range(BLOCKS):
            f_gate(b)
        unit(2, 1, "vv")
        unit(3, 0, "ss")
        unit(3, 1, "ss")
        halves = [slice(h * 256, (h + 1) * 256) for h in range(2)]
        for b in range(BLOCKS):
            keep_old(b)
        for b in range(BLOCKS):
            for c in halves:
                admit_new(b, c)
            for c in halves:
                blend(b, c)
        for b in range(BLOCKS):
            r_gate(b)
            for c in halves:
                squash(b, c)
        for b in range(BLOCKS):
            for c in halves:
                finish(b, c)
                store(b, c)
